import numpy as np, ml_dtypes
CORES = [4,20,60,84,92,100,116]
N = 7
TK = 512
COEF = [[3,1,1,1,1,1,1],[1,3,1,1,1,1,1],[1,1,3,1,1,1,1],[1,1,1,3,1,1,1],[1,1,1,1,3,1,1],[1,1,1,1,1,3,1],[1,1,1,1,1,1,3]]
def setup_inputs(rng):
    return {"x": rng.standard_normal((N, 128, TK), dtype=np.float32).astype(ml_dtypes.bfloat16), "a": (rng.standard_normal((N, 128, 128), dtype=np.float32) / 11).astype(ml_dtypes.bfloat16)}
def setup_inputs_big(rng):
    d = setup_inputs(rng)
    for k in ("x", "a"): d[k] = (d[k].astype(np.float32) * 1024.0).astype(d[k].dtype)
    return d
def setup_inputs_small(rng):
    d = setup_inputs(rng)
    for k in ("x", "a"): d[k] = (d[k].astype(np.float32) * (1 / 1024.0)).astype(d[k].dtype)
    return d
def setup_inputs_apart(rng):
    d = setup_inputs(rng)
    f = (10.0 ** rng.permutation(np.linspace(-1.5, 1.5, N))).astype(np.float32).reshape(N, 1, 1)
    for k in ("x", "a"): d[k] = (d[k].astype(np.float32) * f).astype(d[k].dtype)
    return d
def reference(x, a):
    X, A = x.astype(np.float64), a.astype(np.float64)
    y = np.stack([A[r].T @ sum(COEF[r][j] * X[j] for j in range(N)) for r in range(N)])
    return {"y": y.astype(ml_dtypes.bfloat16)}

@@ -1,0 +1,153 @@
+from concourse.bass import DstId, RemoteDMATransfer
+
+K = 8
+COLS = 512
+PW = COLS // K
+HALVES = 2
+HW = COLS // HALVES
+
+SCRATCH = {
+    "xs": ("dram", [K, 128, PW], "bfloat16"),
+    "land": ("dram", [7, 128, PW], "bfloat16"),
+    "s0": ("dram", [K, 128, PW], "bfloat16"),
+    "s1": ("dram", [K, 128, PW], "bfloat16"),
+    "x_sb": ("sbuf", [128, COLS], "bfloat16"),
+    "a_sb": ("sbuf", [128, 128], "bfloat16"),
+    "s0_sb": ("sbuf", [128, COLS], "bfloat16"),
+    "s1_sb": ("sbuf", [128, COLS], "bfloat16"),
+    "y_sb": ("sbuf", [128, COLS], "bfloat16"),
+    "ps0": ("psum", [128, 512], "float32"),
+    "ps1": ("psum", [128, 512], "float32"),
+}
+SEMAPHORES = ["staged", "sent", "arrived", "sum0", "sum1", "ready", "in0", "in1",
+              "mm0", "mm1", "cp0", "cp1", "st0", "st1"]
+
+
+def _engines(mask):
+    return [1 << b for b in range(mask.bit_length()) if (mask >> b) & 1]
+
+
+def _common_mask(topo, src, dsts):
+    m = topo.mask(src, dsts[0])
+    for d in dsts[1:]:
+        m &= topo.mask(src, d)
+    return m
+
+
+def _plan(T, topo):
+    ranks = list(T.cores)
+    groups = []
+    for c in ranks:
+        for grp in groups:
+            if topo.may_write(c, grp[0]) and topo.may_write(grp[0], c):
+                grp.append(c)
+                break
+        else:
+            groups.append([c])
+    groups.sort(key=len, reverse=True)
+    assert len(groups) == 2
+    home = topo.die(ranks[0])
+    reducers = []
+    for gi, grp in enumerate(groups):
+        by_chip = {}
+        for h in range(topo.CHIPS * topo.CORES_PER_CHIP):
+            if h in ranks:
+                continue
+            if not all(topo.may_write(c, h) for c in grp):
+                continue
+            if not all(topo.may_write(h, d) for d in ranks):
+                continue
+            if (topo.die(h) == home) != (gi == 0):
+                continue
+            by_chip.setdefault(topo.chip(h), h)
+        reds = [by_chip[ch] for ch in sorted(by_chip)][:K]
+        assert len(reds) == K
+        reducers.append(reds)
+    return groups, reducers
+
+
+def _dst(topo, c):
+    rid, pid, _ = topo.addr(c)
+    return DstId(rid=rid, pnc=pid)
+
+
+def _reducer(g, core, T, topo, gi, p, grp):
+    ranks = list(T.cores)
+    mask = _common_mask(topo, core, ranks)
+    g.wait_ge(T.sem.arrived, len(grp))
+    g.remote_dma_fused(
+        [RemoteDMATransfer(dst_ids=[_dst(topo, d) for d in ranks],
+                           dma_engine_mask=mask,
+                           remote_sem=T.sem["sum%d" % gi],
+                           srcs=[T.land[i] for i in range(len(grp))],
+                           dsts=[T["s%d" % gi][p] for _ in ranks],
+                           alu_op=1)],
+        local_sem=T.sem.sent)
+    g.wait_ge(T.sem.sent, len(_engines(mask)))
+
+
+def rank_program(g, core, T, topo):
+    groups, reducers = _plan(T, topo)
+    ranks = list(T.cores)
+    rank = T.rank_of(core)
+    if rank is None:
+        for gi, reds in enumerate(reducers):
+            if core in reds:
+                _reducer(g, core, T, topo, gi, reds.index(core), groups[gi])
+        return
+
+    coef = T.tables["COEF"][rank]
+    off = [coef[j] for j in range(len(ranks)) if j != rank]
+    base = off[0]
+    extra = coef[rank] - base
+    assert all(w == base for w in off) and base >= 1 and extra >= 0
+    assert all(T.tables["COEF"][r][j] == base for r in range(len(ranks)) for j in range(len(ranks)) if j != r)
+
+    gi = [i for i, grp in enumerate(groups) if core in grp][0]
+    slot = groups[gi].index(core)
+    reds = reducers[gi]
+
+    g.sync.dma_start(T.xs[:], T.x[:]).then_inc(T.sem.staged, 16)
+    eng = _engines(_common_mask(topo, core, reds))
+    assert len(eng) >= K
+    g.wait_ge(T.sem.staged, 16)
+    g.remote_dma_fused(
+        [RemoteDMATransfer(dst_ids=[_dst(topo, reds[p])], dma_engine_mask=eng[p], remote_sem=T.sem.arrived,
+                           src=T.xs[p], dst=T.land[slot]) for p in range(K)],
+        local_sem=T.sem.sent)
+
+    g.sync.wait_ge(T.sem.sent, K)
+    g.sync.dma_start(T.x_sb[:], T.x[:]).then_inc(T.sem.ready, 16)
+    g.scalar.wait_ge(T.sem.sent, K)
+    g.scalar.dma_start(T.a_sb[:], T.a[:]).then_inc(T.sem.ready, 16)
+
+    n0 = K * len(_engines(_common_mask(topo, reducers[0][0], ranks)))
+    n1 = K * len(_engines(_common_mask(topo, reducers[1][0], ranks)))
+    g.sync.wait_ge(T.sem.sum0, n0)
+    g.sync.dma_start(T.s0_sb[:], T.s0[:]).then_inc(T.sem.in0, 16)
+    g.scalar.wait_ge(T.sem.sum1, n1)
+    g.scalar.dma_start(T.s1_sb[:], T.s1[:]).then_inc(T.sem.in1, 16)
+
+    terms = [(T.sem.ready, 32, T.x_sb, extra), (T.sem.in1, 16, T.s1_sb, base), (T.sem.in0, 16, T.s0_sb, base)]
+    terms = [t for t in terms if t[3] > 0]
+    ps = [T.ps0, T.ps1]
+    if extra == 0:
+        g.tensor.wait_ge(T.sem.ready, 32)
+    for ti, (sem, val, buf, times) in enumerate(terms):
+        g.tensor.wait_ge(sem, val)
+        for h in range(HALVES):
+            for k in range(times):
+                first = ti == 0 and k == 0
+                last = ti == len(terms) - 1 and k == times - 1
+                mm = g.tensor.matmul(ps[h][:, 0:HW], T.a_sb[:], buf[:, h * HW:(h + 1) * HW], first, last)
+                if last:
+                    mm.then_inc(T.sem["mm%d" % h], 1)
+
+    queues = [g.sync, g.scalar]
+    for h in range(HALVES):
+        g.vector.wait_ge(T.sem["mm%d" % h], 1)
+        g.vector.tensor_copy(T.y_sb[:, h * HW:(h + 1) * HW], ps[h][:, 0:HW]).then_inc(T.sem["cp%d" % h], 1)
+        q = queues[h]
+        q.wait_ge(T.sem["cp%d" % h], 1)
+        q.dma_start(T.y[:, h * HW:(h + 1) * HW], T.y_sb[:, h * HW:(h + 1) * HW]).then_inc(T.sem["st%d" % h], 16)
+        q.wait_ge(T.sem["st%d" % h], 16)

@@ -1,16 +1,23 @@
 from concourse.bass import DstId, RemoteDMATransfer
 
-K = 8
+WAVES = 2
+PER_WAVE = 8
+PIECES = WAVES * PER_WAVE
+NRED = min(PIECES, 16)
+ROUNDS = PIECES // NRED
 COLS = 512
-PW = COLS // K
+PW = COLS // PIECES
+RP = 128 // WAVES
 HALVES = 2
 HW = COLS // HALVES
+NRANKS = 7
+ROTATE = False
 
 SCRATCH = {
-    "xs": ("dram", [K, 128, PW], "bfloat16"),
-    "land": ("dram", [7, 128, PW], "bfloat16"),
-    "s0": ("dram", [K, 128, PW], "bfloat16"),
-    "s1": ("dram", [K, 128, PW], "bfloat16"),
+    "xs": ("dram", [PIECES, 128, PW], "bfloat16"),
+    "land": ("dram", [ROUNDS * NRANKS, 128, PW], "bfloat16"),
+    "s0": ("dram", [PIECES, 128, PW], "bfloat16"),
+    "s1": ("dram", [PIECES, 128, PW], "bfloat16"),
     "x_sb": ("sbuf", [128, COLS], "bfloat16"),
     "a_sb": ("sbuf", [128, 128], "bfloat16"),
     "s0_sb": ("sbuf", [128, COLS], "bfloat16"),
@@ -19,8 +26,11 @@ SCRATCH = {
     "ps0": ("psum", [128, 512], "float32"),
     "ps1": ("psum", [128, 512], "float32"),
 }
-SEMAPHORES = ["staged", "sent", "arrived", "sum0", "sum1", "ready", "in0", "in1",
-              "mm0", "mm1", "cp0", "cp1", "st0", "st1"]
+SEMAPHORES = (["sent", "ready", "pe", "mm0", "mm1", "cp0", "cp1", "st0", "st1"]
+              + ["arr%d" % j for j in range(ROUNDS)]
+              + ["staged%d" % w for w in range(WAVES)]
+              + ["sum%d_%d" % (gi, w) for gi in range(2) for w in range(WAVES)]
+              + ["in%d_%d" % (gi, w) for gi in range(2) for w in range(WAVES)])
 
 
 def _engines(mask):
@@ -59,9 +69,10 @@ def _plan(T, topo):
                 continue
             if (topo.die(h) == home) != (gi == 0):
                 continue
-            by_chip.setdefault(topo.chip(h), h)
-        reds = [by_chip[ch] for ch in sorted(by_chip)][:K]
-        assert len(reds) == K
+            by_chip.setdefault(topo.chip(h), []).append(h)
+        depth = max(len(v) for v in by_chip.values())
+        reds = [by_chip[ch][i] for i in range(depth) for ch in sorted(by_chip) if i < len(by_chip[ch])][:NRED]
+        assert len(reds) == NRED
         reducers.append(reds)
     return groups, reducers
 
@@ -71,19 +82,24 @@ def _dst(topo, c):
     return DstId(rid=rid, pnc=pid)
 
 
-def _reducer(g, core, T, topo, gi, p, grp):
+def _reducer(g, core, T, topo, gi, q, grp):
     ranks = list(T.cores)
     mask = _common_mask(topo, core, ranks)
-    g.wait_ge(T.sem.arrived, len(grp))
-    g.remote_dma_fused(
-        [RemoteDMATransfer(dst_ids=[_dst(topo, d) for d in ranks],
-                           dma_engine_mask=mask,
-                           remote_sem=T.sem["sum%d" % gi],
-                           srcs=[T.land[i] for i in range(len(grp))],
-                           dsts=[T["s%d" % gi][p] for _ in ranks],
-                           alu_op=1)],
-        local_sem=T.sem.sent)
-    g.wait_ge(T.sem.sent, len(_engines(mask)))
+    if ROTATE:
+        r = q % len(ranks)
+        ranks = ranks[r:] + ranks[:r]
+    for j in range(ROUNDS):
+        p = q + j * NRED
+        g.wait_ge(T.sem["arr%d" % j], len(grp))
+        g.remote_dma_fused(
+            [RemoteDMATransfer(dst_ids=[_dst(topo, d) for d in ranks],
+                               dma_engine_mask=mask,
+                               remote_sem=T.sem["sum%d_%d" % (gi, p // PER_WAVE)],
+                               srcs=[T.land[j * NRANKS + i] for i in range(len(grp))],
+                               dsts=[T["s%d" % gi][p] for _ in ranks],
+                               alu_op=1)],
+            local_sem=T.sem.sent)
+    g.wait_ge(T.sem.sent, ROUNDS * len(_engines(mask)))
 
 
 def rank_program(g, core, T, topo):
@@ -106,44 +122,58 @@ def rank_program(g, core, T, topo):
     gi = [i for i, grp in enumerate(groups) if core in grp][0]
     slot = groups[gi].index(core)
     reds = reducers[gi]
+    queues = [g.sync, g.scalar]
 
-    g.sync.dma_start(T.xs[:], T.x[:]).then_inc(T.sem.staged, 16)
+    for w in range(WAVES):
+        queues[w % 2].dma_start(T.xs[w * PER_WAVE:(w + 1) * PER_WAVE], T.x[w * RP:(w + 1) * RP, :]).then_inc(
+            T.sem["staged%d" % w], 16)
     eng = _engines(_common_mask(topo, core, reds))
-    assert len(eng) >= K
-    g.wait_ge(T.sem.staged, 16)
-    g.remote_dma_fused(
-        [RemoteDMATransfer(dst_ids=[_dst(topo, reds[p])], dma_engine_mask=eng[p], remote_sem=T.sem.arrived,
-                           src=T.xs[p], dst=T.land[slot]) for p in range(K)],
-        local_sem=T.sem.sent)
+    assert len(eng) >= PER_WAVE
+    for w in range(WAVES):
+        g.wait_ge(T.sem["staged%d" % w], 16)
+        g.remote_dma_fused(
+            [RemoteDMATransfer(dst_ids=[_dst(topo, reds[p % NRED])], dma_engine_mask=eng[p % PER_WAVE],
+                               remote_sem=T.sem["arr%d" % (p // NRED)],
+                               src=T.xs[p], dst=T.land[(p // NRED) * NRANKS + slot])
+             for p in range(w * PER_WAVE, (w + 1) * PER_WAVE)],
+            local_sem=T.sem.sent)
 
-    g.sync.wait_ge(T.sem.sent, K)
+    g.sync.wait_ge(T.sem.sent, PIECES)
     g.sync.dma_start(T.x_sb[:], T.x[:]).then_inc(T.sem.ready, 16)
-    g.scalar.wait_ge(T.sem.sent, K)
+    g.scalar.wait_ge(T.sem.sent, PIECES)
     g.scalar.dma_start(T.a_sb[:], T.a[:]).then_inc(T.sem.ready, 16)
 
-    n0 = K * len(_engines(_common_mask(topo, reducers[0][0], ranks)))
-    n1 = K * len(_engines(_common_mask(topo, reducers[1][0], ranks)))
-    g.sync.wait_ge(T.sem.sum0, n0)
-    g.sync.dma_start(T.s0_sb[:], T.s0[:]).then_inc(T.sem.in0, 16)
-    g.scalar.wait_ge(T.sem.sum1, n1)
-    g.scalar.dma_start(T.s1_sb[:], T.s1[:]).then_inc(T.sem.in1, 16)
+    for k in range(2):
+        landed = PER_WAVE * len(_engines(_common_mask(topo, reducers[k][0], ranks)))
+        for w in range(WAVES):
+            queues[k].wait_ge(T.sem["sum%d_%d" % (k, w)], landed)
+            queues[k].dma_start(T["s%d_sb" % k][w * RP:(w + 1) * RP, :],
+                                T["s%d" % k][w * PER_WAVE:(w + 1) * PER_WAVE]).then_inc(T.sem["in%d_%d" % (k, w)], 16)
 
-    terms = [(T.sem.ready, 32, T.x_sb, extra), (T.sem.in1, 16, T.s1_sb, base), (T.sem.in0, 16, T.s0_sb, base)]
-    terms = [t for t in terms if t[3] > 0]
+    blocks = [[(T.sem.ready, 32, T.x_sb, 0, 128, extra)]]
+    for w in range(WAVES):
+        blocks.append([(T.sem["in%d_%d" % (k, w)], 16, T["s%d_sb" % k], w * RP, (w + 1) * RP, base) for k in (1, 0)])
     ps = [T.ps0, T.ps1]
-    if extra == 0:
-        g.tensor.wait_ge(T.sem.ready, 32)
-    for ti, (sem, val, buf, times) in enumerate(terms):
-        g.tensor.wait_ge(sem, val)
-        for h in range(HALVES):
-            for k in range(times):
-                first = ti == 0 and k == 0
-                last = ti == len(terms) - 1 and k == times - 1
-                mm = g.tensor.matmul(ps[h][:, 0:HW], T.a_sb[:], buf[:, h * HW:(h + 1) * HW], first, last)
-                if last:
-                    mm.then_inc(T.sem["mm%d" % h], 1)
+    started = [False] * HALVES
+    fenced = 0
+    for bi, block in enumerate(blocks):
+        for ti, (sem, val, buf, lo, hi, times) in enumerate(block):
+            g.tensor.wait_ge(sem, val)
+            if ti == 0 and fenced:
+                g.tensor.wait_ge(T.sem.pe, fenced)
+            for h in range(HALVES):
+                for k in range(times):
+                    closes = ti == len(block) - 1 and k == times - 1
+                    last = closes and bi == len(blocks) - 1
+                    mm = g.tensor.matmul(ps[h][:, 0:HW], T.a_sb[lo:hi, :], buf[lo:hi, h * HW:(h + 1) * HW],
+                                         not started[h], last)
+                    started[h] = True
+                    if last:
+                        mm.then_inc(T.sem["mm%d" % h], 1)
+                    elif closes:
+                        mm.then_inc(T.sem.pe, 1)
+                        fenced += 1
 
-    queues = [g.sync, g.scalar]
     for h in range(HALVES):
         g.vector.wait_ge(T.sem["mm%d" % h], 1)
         g.vector.tensor_copy(T.y_sb[:, h * HW:(h + 1) * HW], ps[h][:, 0:HW]).then_inc(T.sem["cp%d" % h], 1)

@@ -1,36 +1,35 @@
 from concourse.bass import DstId, RemoteDMATransfer
 
-WAVES = 2
-PER_WAVE = 8
-PIECES = WAVES * PER_WAVE
-NRED = min(PIECES, 16)
-ROUNDS = PIECES // NRED
 COLS = 512
-PW = COLS // PIECES
-RP = 128 // WAVES
+PER_SEG = 8
+SEG_ROWS = [64, 32, 32]
+SEG_BUF = ["A", "B", "B"]
+SEG_SLOT = [0, 0, PER_SEG]
+PW = {"A": 32, "B": 16}
+NSEG = len(SEG_ROWS)
 HALVES = 2
 HW = COLS // HALVES
 NRANKS = 7
-ROTATE = False
 
 SCRATCH = {
-    "xs": ("dram", [PIECES, 128, PW], "bfloat16"),
-    "land": ("dram", [ROUNDS * NRANKS, 128, PW], "bfloat16"),
-    "s0": ("dram", [PIECES, 128, PW], "bfloat16"),
-    "s1": ("dram", [PIECES, 128, PW], "bfloat16"),
+    "xsA": ("dram", [PER_SEG, 128, PW["A"]], "bfloat16"),
+    "xsB": ("dram", [2 * PER_SEG, 128, PW["B"]], "bfloat16"),
+    "landA": ("dram", [NRANKS, 128, PW["A"]], "bfloat16"),
+    "landB": ("dram", [NRANKS, 128, PW["B"]], "bfloat16"),
+    "s0A": ("dram", [PER_SEG, 128, PW["A"]], "bfloat16"),
+    "s0B": ("dram", [2 * PER_SEG, 128, PW["B"]], "bfloat16"),
+    "s1A": ("dram", [PER_SEG, 128, PW["A"]], "bfloat16"),
+    "s1B": ("dram", [2 * PER_SEG, 128, PW["B"]], "bfloat16"),
     "x_sb": ("sbuf", [128, COLS], "bfloat16"),
     "a_sb": ("sbuf", [128, 128], "bfloat16"),
-    "s0_sb": ("sbuf", [128, COLS], "bfloat16"),
-    "s1_sb": ("sbuf", [128, COLS], "bfloat16"),
+    "z0": ("sbuf", [128, COLS], "bfloat16"),
+    "z1": ("sbuf", [128, COLS], "bfloat16"),
     "y_sb": ("sbuf", [128, COLS], "bfloat16"),
     "ps0": ("psum", [128, 512], "float32"),
     "ps1": ("psum", [128, 512], "float32"),
 }
-SEMAPHORES = (["sent", "ready", "pe", "mm0", "mm1", "cp0", "cp1", "st0", "st1"]
-              + ["arr%d" % j for j in range(ROUNDS)]
-              + ["staged%d" % w for w in range(WAVES)]
-              + ["sum%d_%d" % (gi, w) for gi in range(2) for w in range(WAVES)]
-              + ["in%d_%d" % (gi, w) for gi in range(2) for w in range(WAVES)])
+SEMAPHORES = (["sent", "arrived", "ready", "staged0", "staged1", "in0", "in1", "mm0", "mm1", "cp0", "cp1", "st0", "st1"]
+              + ["sum%d_%d" % (k, s) for k in range(2) for s in range(NSEG)])
 
 
 def _engines(mask):
@@ -42,6 +41,10 @@ def _common_mask(topo, src, dsts):
     for d in dsts[1:]:
         m &= topo.mask(src, d)
     return m
+
+
+def _seg_start(k, s):
+    return (SEG_ROWS[0] * k + sum(SEG_ROWS[:s])) % 128
 
 
 def _plan(T, topo):
@@ -56,10 +59,9 @@ def _plan(T, topo):
             groups.append([c])
     groups.sort(key=len, reverse=True)
     assert len(groups) == 2
-    home = topo.die(ranks[0])
     reducers = []
-    for gi, grp in enumerate(groups):
-        by_chip = {}
+    for k, grp in enumerate(groups):
+        by_die = {}
         for h in range(topo.CHIPS * topo.CORES_PER_CHIP):
             if h in ranks:
                 continue
@@ -67,13 +69,15 @@ def _plan(T, topo):
                 continue
             if not all(topo.may_write(h, d) for d in ranks):
                 continue
-            if (topo.die(h) == home) != (gi == 0):
-                continue
-            by_chip.setdefault(topo.chip(h), []).append(h)
-        depth = max(len(v) for v in by_chip.values())
-        reds = [by_chip[ch][i] for i in range(depth) for ch in sorted(by_chip) if i < len(by_chip[ch])][:NRED]
-        assert len(reds) == NRED
-        reducers.append(reds)
+            by_die.setdefault(topo.die(h), {}).setdefault(topo.chip(h), []).append(h)
+        dies = sorted(by_die)
+        assert len(dies) == 2
+        first, later = by_die[dies[k]], by_die[dies[1 - k]]
+        segs = [[first[ch][0] for ch in sorted(first)][:PER_SEG]]
+        for i in range(NSEG - 1):
+            segs.append([later[ch][i] for ch in sorted(later)][:PER_SEG])
+        assert all(len(sg) == PER_SEG for sg in segs)
+        reducers.append(segs)
     return groups, reducers
 
 
@@ -82,24 +86,21 @@ def _dst(topo, c):
     return DstId(rid=rid, pnc=pid)
 
 
-def _reducer(g, core, T, topo, gi, q, grp):
+def _reducer(g, core, T, topo, k, s, i, grp):
     ranks = list(T.cores)
     mask = _common_mask(topo, core, ranks)
-    if ROTATE:
-        r = q % len(ranks)
-        ranks = ranks[r:] + ranks[:r]
-    for j in range(ROUNDS):
-        p = q + j * NRED
-        g.wait_ge(T.sem["arr%d" % j], len(grp))
-        g.remote_dma_fused(
-            [RemoteDMATransfer(dst_ids=[_dst(topo, d) for d in ranks],
-                               dma_engine_mask=mask,
-                               remote_sem=T.sem["sum%d_%d" % (gi, p // PER_WAVE)],
-                               srcs=[T.land[j * NRANKS + i] for i in range(len(grp))],
-                               dsts=[T["s%d" % gi][p] for _ in ranks],
-                               alu_op=1)],
-            local_sem=T.sem.sent)
-    g.wait_ge(T.sem.sent, ROUNDS * len(_engines(mask)))
+    land = T["land" + SEG_BUF[s]]
+    out = T["s%d%s" % (k, SEG_BUF[s])][SEG_SLOT[s] + i]
+    g.wait_ge(T.sem.arrived, len(grp))
+    g.remote_dma_fused(
+        [RemoteDMATransfer(dst_ids=[_dst(topo, d) for d in ranks],
+                           dma_engine_mask=mask,
+                           remote_sem=T.sem["sum%d_%d" % (k, s)],
+                           srcs=[land[j] for j in range(len(grp))],
+                           dsts=[out for _ in ranks],
+                           alu_op=1)],
+        local_sem=T.sem.sent)
+    g.wait_ge(T.sem.sent, len(_engines(mask)))
 
 
 def rank_program(g, core, T, topo):
@@ -107,9 +108,10 @@ def rank_program(g, core, T, topo):
     ranks = list(T.cores)
     rank = T.rank_of(core)
     if rank is None:
-        for gi, reds in enumerate(reducers):
-            if core in reds:
-                _reducer(g, core, T, topo, gi, reds.index(core), groups[gi])
+        for k in range(2):
+            for s in range(NSEG):
+                if core in reducers[k][s]:
+                    _reducer(g, core, T, topo, k, s, reducers[k][s].index(core), groups[k])
         return
 
     coef = T.tables["COEF"][rank]
@@ -121,58 +123,51 @@ def rank_program(g, core, T, topo):
 
     gi = [i for i, grp in enumerate(groups) if core in grp][0]
     slot = groups[gi].index(core)
-    reds = reducers[gi]
     queues = [g.sync, g.scalar]
 
-    for w in range(WAVES):
-        queues[w % 2].dma_start(T.xs[w * PER_WAVE:(w + 1) * PER_WAVE], T.x[w * RP:(w + 1) * RP, :]).then_inc(
-            T.sem["staged%d" % w], 16)
-    eng = _engines(_common_mask(topo, core, reds))
-    assert len(eng) >= PER_WAVE
-    for w in range(WAVES):
-        g.wait_ge(T.sem["staged%d" % w], 16)
+    lo = _seg_start(gi, 0)
+    g.sync.dma_start(T.xsA[:], T.x[lo:lo + SEG_ROWS[0], :]).then_inc(T.sem.staged0, 16)
+    lo = _seg_start(gi, 1)
+    g.scalar.dma_start(T.xsB[:], T.x[lo:lo + SEG_ROWS[1] + SEG_ROWS[2], :]).then_inc(T.sem.staged1, 16)
+
+    for s in range(NSEG):
+        if s < 2:
+            g.wait_ge(T.sem["staged%d" % s], 16)
+        reds = reducers[gi][s]
+        eng = _engines(_common_mask(topo, core, reds))
         g.remote_dma_fused(
-            [RemoteDMATransfer(dst_ids=[_dst(topo, reds[p % NRED])], dma_engine_mask=eng[p % PER_WAVE],
-                               remote_sem=T.sem["arr%d" % (p // NRED)],
-                               src=T.xs[p], dst=T.land[(p // NRED) * NRANKS + slot])
-             for p in range(w * PER_WAVE, (w + 1) * PER_WAVE)],
+            [RemoteDMATransfer(dst_ids=[_dst(topo, reds[i])], dma_engine_mask=eng[i], remote_sem=T.sem.arrived,
+                               src=T["xs" + SEG_BUF[s]][SEG_SLOT[s] + i], dst=T["land" + SEG_BUF[s]][slot])
+             for i in range(PER_SEG)],
             local_sem=T.sem.sent)
 
-    g.sync.wait_ge(T.sem.sent, PIECES)
+    g.sync.wait_ge(T.sem.sent, NSEG * PER_SEG)
     g.sync.dma_start(T.x_sb[:], T.x[:]).then_inc(T.sem.ready, 16)
-    g.scalar.wait_ge(T.sem.sent, PIECES)
+    g.scalar.wait_ge(T.sem.sent, NSEG * PER_SEG)
     g.scalar.dma_start(T.a_sb[:], T.a[:]).then_inc(T.sem.ready, 16)
 
+    z = [T.z0, T.z1, T.z1]
+    zsem = [T.sem.in0, T.sem.in1, T.sem.in1]
     for k in range(2):
-        landed = PER_WAVE * len(_engines(_common_mask(topo, reducers[k][0], ranks)))
-        for w in range(WAVES):
-            queues[k].wait_ge(T.sem["sum%d_%d" % (k, w)], landed)
-            queues[k].dma_start(T["s%d_sb" % k][w * RP:(w + 1) * RP, :],
-                                T["s%d" % k][w * PER_WAVE:(w + 1) * PER_WAVE]).then_inc(T.sem["in%d_%d" % (k, w)], 16)
+        for s in range(NSEG):
+            landed = PER_SEG * len(_engines(_common_mask(topo, reducers[k][s][0], ranks)))
+            lo = _seg_start(k, s)
+            queues[k].wait_ge(T.sem["sum%d_%d" % (k, s)], landed)
+            queues[k].dma_start(z[s][lo:lo + SEG_ROWS[s], :],
+                                T["s%d%s" % (k, SEG_BUF[s])][SEG_SLOT[s]:SEG_SLOT[s] + PER_SEG]).then_inc(zsem[s], 16)
 
-    blocks = [[(T.sem.ready, 32, T.x_sb, 0, 128, extra)]]
-    for w in range(WAVES):
-        blocks.append([(T.sem["in%d_%d" % (k, w)], 16, T["s%d_sb" % k], w * RP, (w + 1) * RP, base) for k in (1, 0)])
+    terms = [(T.sem.ready, 32, T.x_sb, extra), (T.sem.in0, 32, T.z0, base), (T.sem.in1, 64, T.z1, base)]
     ps = [T.ps0, T.ps1]
     started = [False] * HALVES
-    fenced = 0
-    for bi, block in enumerate(blocks):
-        for ti, (sem, val, buf, lo, hi, times) in enumerate(block):
-            g.tensor.wait_ge(sem, val)
-            if ti == 0 and fenced:
-                g.tensor.wait_ge(T.sem.pe, fenced)
-            for h in range(HALVES):
-                for k in range(times):
-                    closes = ti == len(block) - 1 and k == times - 1
-                    last = closes and bi == len(blocks) - 1
-                    mm = g.tensor.matmul(ps[h][:, 0:HW], T.a_sb[lo:hi, :], buf[lo:hi, h * HW:(h + 1) * HW],
-                                         not started[h], last)
-                    started[h] = True
-                    if last:
-                        mm.then_inc(T.sem["mm%d" % h], 1)
-                    elif closes:
-                        mm.then_inc(T.sem.pe, 1)
-                        fenced += 1
+    for ti, (sem, val, buf, times) in enumerate(terms):
+        g.tensor.wait_ge(sem, val)
+        for h in range(HALVES):
+            for k in range(times):
+                last = ti == len(terms) - 1 and k == times - 1
+                mm = g.tensor.matmul(ps[h][:, 0:HW], T.a_sb[:], buf[:, h * HW:(h + 1) * HW], not started[h], last)
+                started[h] = True
+                if last:
+                    mm.then_inc(T.sem["mm%d" % h], 1)
 
     for h in range(HALVES):
         g.vector.wait_ge(T.sem["mm%d" % h], 1)

from concourse.bass import DstId, RemoteDMATransfer

COLS = 512
PER_SEG = 8
SEG_ROWS = [64, 32, 32]
SEG_BUF = ["A", "B", "B"]
SEG_SLOT = [0, 0, PER_SEG]
PW = {"A": 32, "B": 16}
NSEG = len(SEG_ROWS)
HALVES = 2
HW = COLS // HALVES
NRANKS = 7

SCRATCH = {
    "xsA": ("dram", [PER_SEG, 128, PW["A"]], "bfloat16"),
    "xsB": ("dram", [2 * PER_SEG, 128, PW["B"]], "bfloat16"),
    "landA": ("dram", [NRANKS, 128, PW["A"]], "bfloat16"),
    "landB": ("dram", [NRANKS, 128, PW["B"]], "bfloat16"),
    "s0A": ("dram", [PER_SEG, 128, PW["A"]], "bfloat16"),
    "s0B": ("dram", [2 * PER_SEG, 128, PW["B"]], "bfloat16"),
    "s1A": ("dram", [PER_SEG, 128, PW["A"]], "bfloat16"),
    "s1B": ("dram", [2 * PER_SEG, 128, PW["B"]], "bfloat16"),
    "x_sb": ("sbuf", [128, COLS], "bfloat16"),
    "a_sb": ("sbuf", [128, 128], "bfloat16"),
    "z0": ("sbuf", [128, COLS], "bfloat16"),
    "z1": ("sbuf", [128, COLS], "bfloat16"),
    "y_sb": ("sbuf", [128, COLS], "bfloat16"),
    "ps0": ("psum", [128, 512], "float32"),
    "ps1": ("psum", [128, 512], "float32"),
}
SEMAPHORES = (["sent", "arrived", "ready", "staged0", "staged1", "in0", "in1", "mm0", "mm1", "cp0", "cp1", "st0", "st1"]
              + ["sum%d_%d" % (k, s) for k in range(2) for s in range(NSEG)])


def _engines(mask):
    return [1 << b for b in range(mask.bit_length()) if (mask >> b) & 1]


def _common_mask(topo, src, dsts):
    m = topo.mask(src, dsts[0])
    for d in dsts[1:]:
        m &= topo.mask(src, d)
    return m


def _seg_start(k, s):
    return (SEG_ROWS[0] * k + sum(SEG_ROWS[:s])) % 128


def _plan(T, topo):
    ranks = list(T.cores)
    groups = []
    for c in ranks:
        for grp in groups:
            if topo.may_write(c, grp[0]) and topo.may_write(grp[0], c):
                grp.append(c)
                break
        else:
            groups.append([c])
    groups.sort(key=len, reverse=True)
    assert len(groups) == 2
    reducers = []
    for k, grp in enumerate(groups):
        by_die = {}
        for h in range(topo.CHIPS * topo.CORES_PER_CHIP):
            if h in ranks:
                continue
            if not all(topo.may_write(c, h) for c in grp):
                continue
            if not all(topo.may_write(h, d) for d in ranks):
                continue
            by_die.setdefault(topo.die(h), {}).setdefault(topo.chip(h), []).append(h)
        dies = sorted(by_die)
        assert len(dies) == 2
        first, later = by_die[dies[k]], by_die[dies[1 - k]]
        segs = [[first[ch][0] for ch in sorted(first)][:PER_SEG]]
        for i in range(NSEG - 1):
            segs.append([later[ch][i] for ch in sorted(later)][:PER_SEG])
        assert all(len(sg) == PER_SEG for sg in segs)
        reducers.append(segs)
    return groups, reducers


def _dst(topo, c):
    rid, pid, _ = topo.addr(c)
    return DstId(rid=rid, pnc=pid)


def _reducer(g, core, T, topo, k, s, i, grp):
    ranks = list(T.cores)
    mask = _common_mask(topo, core, ranks)
    land = T["land" + SEG_BUF[s]]
    out = T["s%d%s" % (k, SEG_BUF[s])][SEG_SLOT[s] + i]
    g.wait_ge(T.sem.arrived, len(grp))
    g.remote_dma_fused(
        [RemoteDMATransfer(dst_ids=[_dst(topo, d) for d in ranks],
                           dma_engine_mask=mask,
                           remote_sem=T.sem["sum%d_%d" % (k, s)],
                           srcs=[land[j] for j in range(len(grp))],
                           dsts=[out for _ in ranks],
                           alu_op=1)],
        local_sem=T.sem.sent)
    g.wait_ge(T.sem.sent, len(_engines(mask)))


def rank_program(g, core, T, topo):
    groups, reducers = _plan(T, topo)
    ranks = list(T.cores)
    rank = T.rank_of(core)
    if rank is None:
        for k in range(2):
            for s in range(NSEG):
                if core in reducers[k][s]:
                    _reducer(g, core, T, topo, k, s, reducers[k][s].index(core), groups[k])
        return

    coef = T.tables["COEF"][rank]
    off = [coef[j] for j in range(len(ranks)) if j != rank]
    base = off[0]
    extra = coef[rank] - base
    assert all(w == base for w in off) and base >= 1 and extra >= 0
    assert all(T.tables["COEF"][r][j] == base for r in range(len(ranks)) for j in range(len(ranks)) if j != r)

    gi = [i for i, grp in enumerate(groups) if core in grp][0]
    slot = groups[gi].index(core)
    queues = [g.sync, g.scalar]

    lo = _seg_start(gi, 0)
    g.sync.dma_start(T.xsA[:], T.x[lo:lo + SEG_ROWS[0], :]).then_inc(T.sem.staged0, 16)
    lo = _seg_start(gi, 1)
    g.scalar.dma_start(T.xsB[:], T.x[lo:lo + SEG_ROWS[1] + SEG_ROWS[2], :]).then_inc(T.sem.staged1, 16)

    for s in range(NSEG):
        if s < 2:
            g.wait_ge(T.sem["staged%d" % s], 16)
        reds = reducers[gi][s]
        eng = _engines(_common_mask(topo, core, reds))
        g.remote_dma_fused(
            [RemoteDMATransfer(dst_ids=[_dst(topo, reds[i])], dma_engine_mask=eng[i], remote_sem=T.sem.arrived,
                               src=T["xs" + SEG_BUF[s]][SEG_SLOT[s] + i], dst=T["land" + SEG_BUF[s]][slot])
             for i in range(PER_SEG)],
            local_sem=T.sem.sent)

    g.sync.wait_ge(T.sem.sent, NSEG * PER_SEG)
    g.sync.dma_start(T.x_sb[:], T.x[:]).then_inc(T.sem.ready, 16)
    g.scalar.wait_ge(T.sem.sent, NSEG * PER_SEG)
    g.scalar.dma_start(T.a_sb[:], T.a[:]).then_inc(T.sem.ready, 16)

    z = [T.z0, T.z1, T.z1]
    zsem = [T.sem.in0, T.sem.in1, T.sem.in1]
    for k in range(2):
        for s in range(NSEG):
            landed = PER_SEG * len(_engines(_common_mask(topo, reducers[k][s][0], ranks)))
            lo = _seg_start(k, s)
            queues[k].wait_ge(T.sem["sum%d_%d" % (k, s)], landed)
            queues[k].dma_start(z[s][lo:lo + SEG_ROWS[s], :],
                                T["s%d%s" % (k, SEG_BUF[s])][SEG_SLOT[s]:SEG_SLOT[s] + PER_SEG]).then_inc(zsem[s], 16)

    terms = [(T.sem.ready, 32, T.x_sb, extra), (T.sem.in0, 32, T.z0, base), (T.sem.in1, 64, T.z1, base)]
    ps = [T.ps0, T.ps1]
    started = [False] * HALVES
    for ti, (sem, val, buf, times) in enumerate(terms):
        g.tensor.wait_ge(sem, val)
        for h in range(HALVES):
            for k in range(times):
                last = ti == len(terms) - 1 and k == times - 1
                mm = g.tensor.matmul(ps[h][:, 0:HW], T.a_sb[:], buf[:, h * HW:(h + 1) * HW], not started[h], last)
                started[h] = True
                if last:
                    mm.then_inc(T.sem["mm%d" % h], 1)

    for h in range(HALVES):
        g.vector.wait_ge(T.sem["mm%d" % h], 1)
        g.vector.tensor_copy(T.y_sb[:, h * HW:(h + 1) * HW], ps[h][:, 0:HW]).then_inc(T.sem["cp%d" % h], 1)
        q = queues[h]
        q.wait_ge(T.sem["cp%d" % h], 1)
        q.dma_start(T.y[:, h * HW:(h + 1) * HW], T.y_sb[:, h * HW:(h + 1) * HW]).then_inc(T.sem["st%d" % h], 16)
        q.wait_ge(T.sem["st%d" % h], 16)
